import numpy as np
import ml_dtypes


def mxq(x, axis, fmt="e4m3"):
    dtype, down = {"e4m3": (ml_dtypes.float8_e4m3fn, 7), "e5m2": (ml_dtypes.float8_e5m2, 14)}[fmt]
    v = np.moveaxis(np.asarray(x, np.float32).astype(ml_dtypes.bfloat16).astype(np.float64), axis, -1)
    blocks = v.reshape(v.shape[:-1] + (-1, 32))
    amax = np.abs(blocks).max(-1, keepdims=True)
    byte = np.maximum(np.where(amax > 0, np.frexp(amax)[1] - 1 + 127, 0) - down, 1)
    scale = np.exp2(byte - 127.0)
    codes = (blocks / scale).astype(np.float32).astype(dtype).astype(np.float64)
    return np.moveaxis((codes * scale).reshape(v.shape), -1, axis)


WIDE = False


def mx_kscale(k):
    if not WIDE:
        return np.ones(k)
    levels = np.array([10, -10, 5, -5, 0])
    if k % 512:
        return np.exp2(np.random.permutation(np.resize(levels, k // 32))).repeat(32)
    a = np.empty((k // 512, 16))
    for p in range(k // 512):
        a[p, :8] = np.random.permutation(np.resize(levels, 8))
        for g in range(8):
            far = levels[np.abs(levels - a[p, g]) >= 10]
            a[p, g + 8] = far[np.random.randint(len(far))]
    return np.exp2(a.ravel()).repeat(32)


def f64(x):
    return np.asarray(x).astype(np.float64)


def striped(idx):
    return np.tile(idx.reshape(-1, 16).T, (8, 1)).astype(np.uint16)


def unstriped(offs):
    return offs[:16].T.reshape(-1).astype(np.int64)


E2M1 = np.array([0.0, 0.5, 1.0, 1.5, 2.0, 3.0, 4.0, 6.0, -0.0, -0.5, -1.0, -1.5, -2.0, -3.0, -4.0, -6.0])


def pack_weight(w, fmt):
    k, n = w.shape
    w = f64(np.asarray(w, np.float32).astype(ml_dtypes.bfloat16)).reshape(k // 32, 32, n)
    amax = np.abs(w).max(1)
    if fmt == "e4m3":
        byte = np.frexp(amax)[1] - 1 + 127 - 7
    else:
        mant, ex = np.frexp(amax / 6.0)
        byte = np.where(mant > 0.5, ex, ex - 1) + 127
    byte = np.clip(np.where(amax > 0, byte, 1), 1, 254)
    scaled = (w * np.exp2(127.0 - byte)[:, None, :]).reshape(k, n).astype(np.float32)
    by_word = np.ascontiguousarray(scaled.reshape(k // 512, 128, 4, n).transpose(0, 1, 3, 2))
    if fmt == "e4m3":
        words = by_word.astype(ml_dtypes.float8_e4m3fn).view(np.uint8)
    else:
        c = by_word.astype(ml_dtypes.float4_e2m1fn).view(np.uint8) & 0xF
        words = (c[..., 0::2] | (c[..., 1::2] << 4)).reshape(k // 512, 128, 2 * n)
    return np.ascontiguousarray(words), np.ascontiguousarray(byte.astype(np.uint8).reshape(k // 512, 16, n))


def unpack_weight(words, scales, fmt):
    g, _, n = scales.shape
    words = np.ascontiguousarray(words).reshape(g, 128, n, -1)
    if fmt == "e4m3":
        vals = words.view(ml_dtypes.float8_e4m3fn).astype(np.float64)
    else:
        nib = np.empty((g, 128, n, 4), np.uint8)
        nib[..., 0::2] = words & 0xF
        nib[..., 1::2] = words >> 4
        vals = E2M1[nib]
    vals = vals * np.repeat(np.exp2(scales.astype(np.float64) - 127.0), 8, axis=1)[..., None]
    return vals.transpose(0, 1, 3, 2).reshape(g * 512, n)


def gelu(v):
    return 0.5 * v * (1.0 + np.tanh(np.sqrt(2.0 / np.pi) * (v + 0.044715 * v**3)))


def bf(x):
    return np.asarray(x, np.float32).astype(ml_dtypes.bfloat16)


def planes(Y):
    n, m = Y.shape
    b = f64(bf(Y)).reshape(n // 32, 32, m)
    amax = np.abs(b).max(1)
    byte = np.clip(np.where(amax > 0, np.frexp(amax)[1] - 1 + 127 - 7, 1), 1, 254)
    codes = (b * np.exp2(127.0 - byte)[:, None, :]).reshape(n, m).astype(np.float32).astype(ml_dtypes.float8_e4m3fn).view(np.uint8)
    words = codes.reshape(n // 512, 128, 4, m).transpose(0, 1, 3, 2)
    return np.ascontiguousarray(words), np.ascontiguousarray(byte.astype(np.uint8).reshape(n // 512, 16, m))


K, T, S, H, P, N, P2 = 1024, 4096, 1024, 1024, 512, 1024, 256

def setup_inputs():
    n = np.random.standard_normal
    s = mx_kscale(K)[:, None]
    u = mx_kscale(H)[:, None]
    size = np.exp(0.8 * n(N))
    tab_words, tab_scales = pack_weight(n((K, T)) * s, "e4m3")
    w2_words, w2_scales = pack_weight(0.75 * n((H, N)) / np.sqrt(H) * size / u, "e2m1")
    return {
        "tab_words": tab_words,
        "tab_scales": tab_scales,
        "offs": striped(np.random.permutation(T)[:S]),
        "pos1": striped(np.random.permutation(S)[:P]),
        "pos2": striped(np.random.permutation(S)[:P]),
        "pos3": striped(np.random.permutation(P)[:P2]),
        "pos4": striped(np.random.permutation(P)[:P2]),
        "w1": (0.5 * n((K, H)) / np.sqrt(K) / s).astype(np.float32),
        "gain": (np.exp(0.3 * n(H)) * np.sqrt(u[:, 0])).astype(np.float32),
        "w2_words": w2_words,
        "w2_scales": w2_scales,
        "pump": (0.5 * n((N, P)) * size[:, None]).astype(np.float32),
    }

def reference(tab_words, tab_scales, offs, pos1, pos2, pos3, pos4, w1, gain, w2_words, w2_scales, pump):
    v = unpack_weight(tab_words, tab_scales, "e4m3")[:, unstriped(offs)]
    q1 = mxq(f64(w1), 0, "e4m3")
    h = f64(gain)[:, None] * np.cos(q1.T @ v)
    z = h[:, unstriped(pos1)] * h[:, unstriped(pos2)]
    w2 = unpack_weight(w2_words, w2_scales, "e2m1")
    e = (w2.T @ mxq(z, 0, "e4m3")) + f64(pump)
    y = np.tanh(e[:, unstriped(pos3)]) - e[:, unstriped(pos4)]
    words, scales = planes(y)
    return y, words, scales

@@ -1,0 +1,286 @@
+import math
+from contextlib import ExitStack
+
+import concourse.mybir as mybir
+
+K, T, S, H, PAIRS, N, P2 = 1024, 4096, 1024, 1024, 512, 1024, 256
+FLOPS = 2 * K * H * S + 2 * H * N * PAIRS
+
+F32 = mybir.dt.float32
+BF16 = mybir.dt.bfloat16
+I32 = mybir.dt.int32
+U32 = mybir.dt.uint32
+U16 = mybir.dt.uint16
+U8 = mybir.dt.uint8
+FP8X4 = mybir.dt.float8_e4m3fn_x4
+FP4X4 = mybir.dt.float4_e2m1fn_x4
+ALU = mybir.AluOpType
+ACT = mybir.ActivationFunctionType
+
+P = 128
+BANK = 512
+
+
+def tile_list_salt_screen_pairs_kernel(
+    tc, tab_words, tab_scales, offs, pos1, pos2, pos3, pos4, w1, gain, w2_words, w2_scales, pump, out_0, out_1, out_2
+):
+    nc = tc.nc
+    with ExitStack() as ctx:
+        keep = ctx.enter_context(tc.tile_pool(name="keep", bufs=1))
+        ring = ctx.enter_context(tc.tile_pool(name="ring", bufs=2))
+        psum = ctx.enter_context(tc.psum_pool(name="psum", bufs=8))
+
+        def held(shape, dtype, name):
+            return keep.tile(shape, dtype, name=name, align_bytes=64)
+
+        def load_list(src, name):
+            tile = held([P, src.shape[1]], U16, name)
+            nc.sync.dma_start(tile[:], src)
+            return tile
+
+        def load_table(a):
+            tile = held([P, T], U32, f"table{a}")
+            nc.sync.dma_start(tile[:].bitcast(I32), tab_words[a].rearrange("p t i -> p (t i)").bitcast(I32))
+            return tile
+
+        def load_w1(b, a, c0, c1):
+            tile = held([P, 4, c1 - c0], F32, f"w1raw{b}{a}{c0}")
+            rows = w1[512 * a : 512 * (a + 1), 512 * b + c0 : 512 * b + c1]
+            nc.sync.dma_start(tile[:], rows.rearrange("(p j) c -> p j c", j=4))
+            return tile
+
+        tab_sc = held([P, T], U8, "tab_sc")
+        w2_sc_raw = held([P, 2 * N], U8, "w2_sc_raw")
+        nc.vector.memset(tab_sc[:].bitcast(I32), 0)
+        nc.vector.memset(w2_sc_raw[:].bitcast(I32), 0)
+        for q in range(4):
+            nc.gpsimd.dma_start(
+                tab_sc[32 * q : 32 * q + 8, :].bitcast(I32), tab_scales[:, 4 * q : 4 * q + 4, :].bitcast(I32)
+            )
+        for q in range(4):
+            nc.gpsimd.dma_start(
+                w2_sc_raw[32 * q : 32 * q + 4, :].bitcast(I32).rearrange("r (a c) -> r a c", a=2),
+                w2_scales[:, 4 * q : 4 * q + 4, :].bitcast(I32).rearrange("a r c -> r a c"),
+            )
+
+        offs_t = load_list(offs, "offs_t")
+        table = [load_table(0), load_table(1)]
+        w1_raw = {(0, 0): [load_w1(0, 0, 0, 512)], (0, 1): [load_w1(0, 1, 0, 256), load_w1(0, 1, 256, 512)]}
+        pos1_t = load_list(pos1, "pos1_t")
+        pos2_t = load_list(pos2, "pos2_t")
+        gain_t = held([P, 2, 4], F32, "gain_t")
+        nc.sync.dma_start(gain_t[:], gain.rearrange("(b p t) -> p b t", b=2, t=4))
+        w1_raw[1, 0] = [load_w1(1, 0, 0, 512)]
+        w2_raw = held([P, 2 * N], U16, "w2_raw")
+        nc.sync.dma_start(
+            w2_raw[:].bitcast(I32).rearrange("p (a c) -> p a c", a=2),
+            w2_words.bitcast(I32).rearrange("a p c -> p a c"),
+        )
+        w1_raw[1, 1] = [load_w1(1, 1, 0, 512)]
+        pos3_t = load_list(pos3, "pos3_t")
+        pos4_t = load_list(pos4, "pos4_t")
+        pump_t = []
+        for g in range(2):
+            tile = held([P, 4 * PAIRS], F32, f"pump{g}")
+            nc.sync.dma_start(tile[:], pump[512 * g : 512 * (g + 1), :].rearrange("(p t) m -> p (t m)", t=4))
+            pump_t.append(tile)
+
+        v_words = [held([P, S], U32, f"v_words{a}") for a in range(2)]
+        v_sc = held([P, S], U8, "v_sc")
+        nc.vector.tensor_copy(v_words[0][:], table[0][:].indirect(offs_t[:]))
+        nc.vector.tensor_copy(v_sc[:], tab_sc[:].indirect(offs_t[:]))
+        nc.vector.tensor_copy(v_words[1][:], table[1][:].indirect(offs_t[:]))
+
+        w2_sc = held([P, 2 * N], U8, "w2_sc")
+        nc.vector.tensor_copy(
+            w2_sc[:].rearrange("p (x t m) -> p x t m", t=4, m=P),
+            w2_sc_raw[:].rearrange("p (x m t) -> p x t m", t=4, m=P),
+        )
+        gain_sq = held([P, 8], F32, "gain_sq")
+        nc.gpsimd.tensor_tensor(
+            gain_sq[:], gain_t[:].rearrange("p b t -> p (b t)"), gain_t[:].rearrange("p b t -> p (b t)"), ALU.mult
+        )
+
+        w1_codes, w1_sc = {}, {}
+
+        def round_w1(b, a):
+            grouped = ring.tile([P, 4 * 512], BF16, name="w1grp", align_bytes=64)
+            dst = grouped[:].rearrange("p (t m j) -> p m t j", t=4, j=4)
+            pieces = w1_raw[b, a]
+            width = P // len(pieces)
+            for i, raw in enumerate(pieces):
+                src = raw[:].rearrange("p j (m t) -> p m t j", t=4)
+                copy = nc.vector.tensor_copy if (i == 1 or b == 1) else nc.scalar.copy
+                copy(dst[:, width * i : width * (i + 1)], src)
+            return grouped
+
+        def quantize_w1(b, a, grouped):
+            w1_codes[b, a] = held([P, 512], U32, f"w1c{b}{a}")
+            w1_sc[b, a] = held([P, 512], U8, f"w1s{b}{a}")
+            nc.vector.quantize_mx(out=w1_codes[b, a][:].bitcast(FP8X4), scales=w1_sc[b, a][:], in_=grouped[:])
+
+        for a in range(2):
+            quantize_w1(0, a, round_w1(0, a))
+
+        z_work = [held([P, 4 * S], F32, f"z_work{b}") for b in range(2)]
+        z_codes = [held([P, PAIRS], U32, f"z_codes{b}") for b in range(2)]
+        z_sc = [held([P, PAIRS], U8, f"z_sc{b}") for b in range(2)]
+        z_grp = [held([P, 4 * PAIRS], BF16, f"z_grp{b}") for b in range(2)]
+        turns, whole, rest, cosine, picked = {}, {}, {}, {}, {}
+
+        def first_product(s):
+            b, t = divmod(s, 4)
+            turns[s] = ring.tile([P, S], F32, name="turns")
+            for half in range(2):
+                cols = slice(BANK * half, BANK * (half + 1))
+                acc = psum.tile([P, BANK], F32, name="acc")
+                for a in range(2):
+                    nc.tensor.matmul_mx(
+                        out=acc[:],
+                        lhsT=w1_codes[b, a][:, P * t : P * (t + 1)].bitcast(FP8X4),
+                        lhsT_scale=w1_sc[b, a][:, P * t : P * (t + 1)],
+                        rhs=v_words[a][:, cols].bitcast(FP8X4),
+                        rhs_scale=v_sc[4 * a : P, cols],
+                        start=(a == 0),
+                        stop=(a == 1),
+                    )
+                nc.scalar.activation(turns[s][:, cols], acc[:], ACT.Abs, scale=0.5 / math.pi)
+
+        def whole_turns(s):
+            slot = (s - 2) % 8
+            whole[s] = z_work[slot // 4][:, S * (slot % 4) : S * (slot % 4 + 1)]
+            nc.scalar.activation(whole[s].bitcast(U32), turns[s][:], ACT.Copy, bias=0.25)
+
+        def remainder(s):
+            rest[s] = ring.tile([P, S], F32, name="rest")
+            nc.vector.scalar_tensor_tensor(
+                rest[s][:], turns[s][:], 0.25, whole[s].bitcast(I32), ALU.add, ALU.subtract
+            )
+
+        def sine(s):
+            cosine[s] = ring.tile([P, S], F32, name="cosine")
+            nc.scalar.activation(cosine[s][:], rest[s][:], ACT.Sin, scale=2.0 * math.pi)
+
+        def pick_screens(s):
+            shallow = ring.tile([P, PAIRS], F32, name="shallow")
+            deep = ring.tile([P, PAIRS], F32, name="deep")
+            nc.vector.tensor_copy(shallow[:], cosine[s][:].indirect(pos1_t[:]))
+            nc.vector.tensor_copy(deep[:], cosine[s][:].indirect(pos2_t[:]))
+            picked[s] = (shallow, deep)
+
+        def pair_product(s):
+            b, t = divmod(s, 4)
+            shallow, deep = picked[s]
+            nc.vector.scalar_tensor_tensor(
+                z_work[b][:, S * t : S * t + PAIRS], shallow[:], gain_sq[:, s : s + 1], deep[:], ALU.mult, ALU.mult
+            )
+
+        def round_z(b, c0, c1, copy):
+            dst = z_grp[b][:, 4 * c0 : 4 * c1].rearrange("p (c i t) -> p c t i", t=4, i=4)
+            src = z_work[b][:].rearrange("p (t m) -> p t m", t=4)[:, :, c0:c1]
+            copy(dst, src.rearrange("p t (c i) -> p c t i", i=4))
+
+        def quantize_z(b):
+            nc.vector.quantize_mx(out=z_codes[b][:].bitcast(FP8X4), scales=z_sc[b][:], in_=z_grp[b][:])
+
+        w2_codes = held([P, 2 * N], U16, "w2_codes")
+        first_product(0)
+        for s in range(-2, 8):
+            if s == -1:
+                sine(0)
+            if s + 2 < 8:
+                whole_turns(s + 2)
+            if 0 < s + 1 < 8:
+                sine(s + 1)
+            if s + 3 < 8:
+                first_product(s + 3)
+            if s >= 0:
+                pick_screens(s)
+            if s + 2 < 8:
+                remainder(s + 2)
+            if s >= 0:
+                pair_product(s)
+            if s == -2:
+                grouped = round_w1(1, 0)
+                nc.vector.tensor_copy(
+                    w2_codes[:].rearrange("p (x t m) -> p x t m", t=4, m=P),
+                    w2_raw[:].rearrange("p (x m t) -> p x t m", t=4, m=P),
+                )
+                quantize_w1(1, 0, grouped)
+            if s == -1:
+                quantize_w1(1, 1, round_w1(1, 1))
+            if s == 3:
+                round_z(0, 0, PAIRS, nc.scalar.copy)
+            if s == 4:
+                quantize_z(0)
+        round_z(1, 0, 256, nc.scalar.copy)
+        round_z(1, 256, PAIRS, nc.vector.tensor_copy)
+        quantize_z(1)
+
+        y32 = [held([P, 4, P2], F32, f"y32_{g}") for g in range(2)]
+
+        def minus_e(s):
+            g, t = divmod(s, 4)
+            acc = psum.tile([P, BANK], F32, name="acc")
+            for a in range(2):
+                cols = slice(N * a + P * s, N * a + P * (s + 1))
+                nc.tensor.matmul_mx(
+                    out=acc[:],
+                    lhsT=w2_codes[:, cols].bitcast(FP4X4),
+                    lhsT_scale=w2_sc[:, cols],
+                    rhs=z_codes[a][:].bitcast(FP8X4),
+                    rhs_scale=z_sc[a][:],
+                    start=(a == 0),
+                    stop=(a == 1),
+                )
+            neg = ring.tile([P, PAIRS], F32, name="neg", bufs=4)
+            nc.vector.scalar_tensor_tensor(
+                neg[:], acc[:], -1.0, pump_t[g][:, PAIRS * t : PAIRS * (t + 1)], ALU.mult, ALU.subtract
+            )
+            return neg
+
+        def bounded(neg):
+            inland = ring.tile([P, P2], F32, name="inland")
+            nc.vector.tensor_copy(inland[:], neg[:].indirect(pos3_t[:]))
+            tanh = ring.tile([P, P2], F32, name="tanh", bufs=3)
+            nc.scalar.activation(tanh[:], inland[:], ACT.Tanh, scale=-1.0)
+            return tanh
+
+        def contrast(s, neg, tanh):
+            g, t = divmod(s, 4)
+            nc.vector.tensor_tensor(y32[g][:, t, :], neg[:].indirect(pos4_t[:]), tanh[:], ALU.add)
+
+        def hand_out(g, copy):
+            nc.sync.dma_start(out_0[512 * g : 512 * (g + 1), :].rearrange("(p t) j -> p t j", t=4), y32[g][:])
+            grouped = held([P, 4 * P2], BF16, f"y_grp{g}")
+            copy(
+                grouped[:].rearrange("p (c i t) -> p c t i", t=4, i=4),
+                y32[g][:].rearrange("p t (c i) -> p c t i", i=4),
+            )
+            return grouped
+
+        def planes(g, grouped):
+            codes = held([P, P2], U32, f"y_codes{g}")
+            scales = held([P, P2], U8, f"y_sc{g}")
+            nc.vector.quantize_mx(out=codes[:].bitcast(FP8X4), scales=scales[:], in_=grouped[:])
+            nc.sync.dma_start(out_1[g].rearrange("p m t -> p (m t)").bitcast(I32), codes[:].bitcast(I32))
+            for q in range(4):
+                queue = nc.scalar if (g == 1 and q >= 2) else nc.sync
+                queue.dma_start(
+                    out_2[g, 4 * q : 4 * q + 4, :].bitcast(I32), scales[32 * q : 32 * q + 4, :].bitcast(I32)
+                )
+
+        negs = {0: minus_e(0), 1: minus_e(1)}
+        tanhs = {0: bounded(negs[0])}
+        grouped0 = None
+        for s in range(8):
+            if s + 2 < 8:
+                negs[s + 2] = minus_e(s + 2)
+            if s + 1 < 8:
+                tanhs[s + 1] = bounded(negs[s + 1])
+            contrast(s, negs[s], tanhs[s])
+            if s == 3:
+                grouped0 = hand_out(0, nc.scalar.copy)
+            if s == 5:
+                planes(0, grouped0)
+        planes(1, hand_out(1, nc.vector.tensor_copy))

@@ -44,10 +44,14 @@ def tile_list_salt_screen_pairs_kernel(
             return tile
 
         def load_w1(b, a, c0, c1):
-            tile = held([P, 4, c1 - c0], F32, f"w1raw{b}{a}{c0}")
+            tile = ring.tile([P, 4, c1 - c0], F32, name="w1raw")
             rows = w1[512 * a : 512 * (a + 1), 512 * b + c0 : 512 * b + c1]
             nc.sync.dma_start(tile[:], rows.rearrange("(p j) c -> p j c", j=4))
             return tile
+
+        warm = held([P, 2], F32, "warm")
+        nc.gpsimd.memset(warm[:, 0:1], 0.0)
+        nc.scalar.activation(warm[:, 1:2], warm[:, 0:1], ACT.Silu)
 
         tab_sc = held([P, T], U8, "tab_sc")
         w2_sc_raw = held([P, 2 * N], U8, "w2_sc_raw")
@@ -57,19 +61,46 @@ def tile_list_salt_screen_pairs_kernel(
             nc.gpsimd.dma_start(
                 tab_sc[32 * q : 32 * q + 8, :].bitcast(I32), tab_scales[:, 4 * q : 4 * q + 4, :].bitcast(I32)
             )
+
+        w1_raw = {(0, 0): [load_w1(0, 0, 0, 512)]}
+        offs_t = load_list(offs, "offs_t")
+        gain_t = held([P, 2, 4], F32, "gain_t")
+        nc.sync.dma_start(gain_t[:], gain.rearrange("(b p t) -> p b t", b=2, t=4))
         for q in range(4):
-            nc.gpsimd.dma_start(
+            nc.sync.dma_start(
                 w2_sc_raw[32 * q : 32 * q + 4, :].bitcast(I32).rearrange("r (a c) -> r a c", a=2),
                 w2_scales[:, 4 * q : 4 * q + 4, :].bitcast(I32).rearrange("a r c -> r a c"),
             )
-
-        offs_t = load_list(offs, "offs_t")
+        w1_raw[0, 1] = [load_w1(0, 1, 0, 512)]
         table = [load_table(0), load_table(1)]
-        w1_raw = {(0, 0): [load_w1(0, 0, 0, 512)], (0, 1): [load_w1(0, 1, 0, 256), load_w1(0, 1, 256, 512)]}
         pos1_t = load_list(pos1, "pos1_t")
         pos2_t = load_list(pos2, "pos2_t")
-        gain_t = held([P, 2, 4], F32, "gain_t")
-        nc.sync.dma_start(gain_t[:], gain.rearrange("(b p t) -> p b t", b=2, t=4))
+
+        v_words = [held([P, S], U32, f"v_words{a}") for a in range(2)]
+        v_sc = held([P, S], U8, "v_sc")
+
+        w1_codes, w1_sc = {}, {}
+
+        def round_w1(b, a):
+            if (b, a) == (1, 1):
+                grouped = keep.tile([P, 4 * 512], BF16, name="w1grp_last", tag="early", align_bytes=64)
+            else:
+                grouped = ring.tile([P, 4 * 512], BF16, name="w1grp", align_bytes=64)
+            dst = grouped[:].rearrange("p (t m j) -> p m t j", t=4, j=4)
+            pieces = w1_raw[b, a]
+            width = P // len(pieces)
+            for i, raw in enumerate(pieces):
+                src = raw[:].rearrange("p j (m t) -> p m t j", t=4)
+                copy = nc.vector.tensor_copy if b == 1 else nc.scalar.copy
+                copy(dst[:, width * i : width * (i + 1)], src)
+            return grouped
+
+        def quantize_w1(b, a, grouped):
+            w1_codes[b, a] = held([P, 512], U32, f"w1c{b}{a}")
+            w1_sc[b, a] = held([P, 512], U8, f"w1s{b}{a}")
+            nc.vector.quantize_mx(out=w1_codes[b, a][:].bitcast(FP8X4), scales=w1_sc[b, a][:], in_=grouped[:])
+
+        grouped = [round_w1(0, a) for a in range(2)]
         w1_raw[1, 0] = [load_w1(1, 0, 0, 512)]
         w2_raw = held([P, 2 * N], U16, "w2_raw")
         nc.sync.dma_start(
@@ -84,43 +115,27 @@ def tile_list_salt_screen_pairs_kernel(
             tile = held([P, 4 * PAIRS], F32, f"pump{g}")
             nc.sync.dma_start(tile[:], pump[512 * g : 512 * (g + 1), :].rearrange("(p t) m -> p (t m)", t=4))
             pump_t.append(tile)
-
-        v_words = [held([P, S], U32, f"v_words{a}") for a in range(2)]
-        v_sc = held([P, S], U8, "v_sc")
-        nc.vector.tensor_copy(v_words[0][:], table[0][:].indirect(offs_t[:]))
-        nc.vector.tensor_copy(v_sc[:], tab_sc[:].indirect(offs_t[:]))
-        nc.vector.tensor_copy(v_words[1][:], table[1][:].indirect(offs_t[:]))
-
+        gain_sq = held([P, 8 * PAIRS], F32, "gain_sq")
+        for s in range(8):
+            nc.scalar.activation(
+                gain_sq[:, PAIRS * s : PAIRS * (s + 1)],
+                gain_t[:, s // 4, s % 4 : s % 4 + 1].to_broadcast([P, PAIRS]),
+                ACT.Square,
+            )
         w2_sc = held([P, 2 * N], U8, "w2_sc")
         nc.vector.tensor_copy(
             w2_sc[:].rearrange("p (x t m) -> p x t m", t=4, m=P),
             w2_sc_raw[:].rearrange("p (x m t) -> p x t m", t=4, m=P),
         )
-        gain_sq = held([P, 8], F32, "gain_sq")
-        nc.gpsimd.tensor_tensor(
-            gain_sq[:], gain_t[:].rearrange("p b t -> p (b t)"), gain_t[:].rearrange("p b t -> p (b t)"), ALU.mult
-        )
-
-        w1_codes, w1_sc = {}, {}
-
-        def round_w1(b, a):
-            grouped = ring.tile([P, 4 * 512], BF16, name="w1grp", align_bytes=64)
-            dst = grouped[:].rearrange("p (t m j) -> p m t j", t=4, j=4)
-            pieces = w1_raw[b, a]
-            width = P // len(pieces)
-            for i, raw in enumerate(pieces):
-                src = raw[:].rearrange("p j (m t) -> p m t j", t=4)
-                copy = nc.vector.tensor_copy if (i == 1 or b == 1) else nc.scalar.copy
-                copy(dst[:, width * i : width * (i + 1)], src)
-            return grouped
-
-        def quantize_w1(b, a, grouped):
-            w1_codes[b, a] = held([P, 512], U32, f"w1c{b}{a}")
-            w1_sc[b, a] = held([P, 512], U8, f"w1s{b}{a}")
-            nc.vector.quantize_mx(out=w1_codes[b, a][:].bitcast(FP8X4), scales=w1_sc[b, a][:], in_=grouped[:])
-
-        for a in range(2):
-            quantize_w1(0, a, round_w1(0, a))
+        quantize_w1(0, 0, grouped[0])
+        nc.vector.tensor_copy(v_sc[:], tab_sc[:].indirect(offs_t[:]))
+        nc.vector.tensor_copy(v_words[0][:], table[0][:].indirect(offs_t[:]))
+        quantize_w1(0, 1, grouped[1])
+        for half in range(2):
+            nc.vector.tensor_copy(
+                v_words[1][:, BANK * half : BANK * (half + 1)],
+                table[1][:].indirect(offs_t[:, 32 * half : 32 * (half + 1)]),
+            )
 
         z_work = [held([P, 4 * S], F32, f"z_work{b}") for b in range(2)]
         z_codes = [held([P, PAIRS], U32, f"z_codes{b}") for b in range(2)]
@@ -147,32 +162,40 @@ def tile_list_salt_screen_pairs_kernel(
                 nc.scalar.activation(turns[s][:, cols], acc[:], ACT.Abs, scale=0.5 / math.pi)
 
         def whole_turns(s):
-            slot = (s - 2) % 8
-            whole[s] = z_work[slot // 4][:, S * (slot % 4) : S * (slot % 4 + 1)]
-            nc.scalar.activation(whole[s].bitcast(U32), turns[s][:], ACT.Copy, bias=0.25)
+            if s == 0:
+                whole[s] = keep.tile([P, S], U32, name="whole_first", tag="early", align_bytes=64)
+            else:
+                whole[s] = ring.tile([P, S], U32, name="whole")
+            nc.scalar.activation(whole[s][:], turns[s][:], ACT.Copy, bias=0.25)
 
         def remainder(s):
-            rest[s] = ring.tile([P, S], F32, name="rest")
+            slot = (s - 1) % 8
+            rest[s] = z_work[slot // 4][:, S * (slot % 4) : S * (slot % 4 + 1)]
             nc.vector.scalar_tensor_tensor(
-                rest[s][:], turns[s][:], 0.25, whole[s].bitcast(I32), ALU.add, ALU.subtract
+                rest[s], turns[s][:], 0.25, whole[s][:].bitcast(I32), ALU.add, ALU.subtract
             )
 
         def sine(s):
-            cosine[s] = ring.tile([P, S], F32, name="cosine")
-            nc.scalar.activation(cosine[s][:], rest[s][:], ACT.Sin, scale=2.0 * math.pi)
+            cosine[s] = ring.tile([P, S], F32, name="cosine", bufs=3)
+            nc.scalar.activation(cosine[s][:], rest[s], ACT.Sin, scale=2.0 * math.pi)
 
-        def pick_screens(s):
-            shallow = ring.tile([P, PAIRS], F32, name="shallow")
-            deep = ring.tile([P, PAIRS], F32, name="deep")
-            nc.vector.tensor_copy(shallow[:], cosine[s][:].indirect(pos1_t[:]))
-            nc.vector.tensor_copy(deep[:], cosine[s][:].indirect(pos2_t[:]))
-            picked[s] = (shallow, deep)
+        def pick(s, c0, c1):
+            tile = ring.tile([P, c1 - c0], F32, name="shallow", bufs=3)
+            nc.vector.tensor_tensor(
+                tile[:],
+                cosine[s][:].indirect(pos1_t[:, c0 // 16 : c1 // 16]),
+                gain_sq[:, PAIRS * s + c0 : PAIRS * s + c1],
+                ALU.mult,
+            )
+            picked[s, c0] = tile
 
-        def pair_product(s):
+        def pair_product(s, c0, c1):
             b, t = divmod(s, 4)
-            shallow, deep = picked[s]
-            nc.vector.scalar_tensor_tensor(
-                z_work[b][:, S * t : S * t + PAIRS], shallow[:], gain_sq[:, s : s + 1], deep[:], ALU.mult, ALU.mult
+            nc.vector.tensor_tensor(
+                z_work[b][:, S * t + c0 : S * t + c1],
+                cosine[s][:].indirect(pos2_t[:, c0 // 16 : c1 // 16]),
+                picked[s, c0][:],
+                ALU.mult,
             )
 
         def round_z(b, c0, c1, copy):
@@ -180,12 +203,14 @@ def tile_list_salt_screen_pairs_kernel(
             src = z_work[b][:].rearrange("p (t m) -> p t m", t=4)[:, :, c0:c1]
             copy(dst, src.rearrange("p t (c i) -> p c t i", i=4))
 
-        def quantize_z(b):
-            nc.vector.quantize_mx(out=z_codes[b][:].bitcast(FP8X4), scales=z_sc[b][:], in_=z_grp[b][:])
+        def quantize_z(b, c0, c1):
+            nc.vector.quantize_mx(
+                out=z_codes[b][:, c0:c1].bitcast(FP8X4), scales=z_sc[b][:, c0:c1], in_=z_grp[b][:, 4 * c0 : 4 * c1]
+            )
 
         w2_codes = held([P, 2 * N], U16, "w2_codes")
         first_product(0)
-        for s in range(-2, 8):
+        for s in range(-2, 7):
             if s == -1:
                 sine(0)
             if s + 2 < 8:
@@ -195,11 +220,11 @@ def tile_list_salt_screen_pairs_kernel(
             if s + 3 < 8:
                 first_product(s + 3)
             if s >= 0:
-                pick_screens(s)
+                pick(s, 0, PAIRS)
+                if s >= 1:
+                    pair_product(s - 1, 0, PAIRS)
             if s + 2 < 8:
                 remainder(s + 2)
-            if s >= 0:
-                pair_product(s)
             if s == -2:
                 grouped = round_w1(1, 0)
                 nc.vector.tensor_copy(
@@ -209,29 +234,36 @@ def tile_list_salt_screen_pairs_kernel(
                 quantize_w1(1, 0, grouped)
             if s == -1:
                 quantize_w1(1, 1, round_w1(1, 1))
-            if s == 3:
+            if s == 5:
                 round_z(0, 0, PAIRS, nc.scalar.copy)
-            if s == 4:
-                quantize_z(0)
+            if s == 6:
+                quantize_z(0, 0, PAIRS)
+        pick(7, 0, 256)
+        pair_product(6, 0, PAIRS)
+        pick(7, 256, PAIRS)
+        pair_product(7, 0, 256)
         round_z(1, 0, 256, nc.scalar.copy)
+        pair_product(7, 256, PAIRS)
         round_z(1, 256, PAIRS, nc.vector.tensor_copy)
-        quantize_z(1)
+        quantize_z(1, 0, 256)
+        quantize_z(1, 256, PAIRS)
 
         y32 = [held([P, 4, P2], F32, f"y32_{g}") for g in range(2)]
 
         def minus_e(s):
             g, t = divmod(s, 4)
             acc = psum.tile([P, BANK], F32, name="acc")
-            for a in range(2):
+            parts = [(0, 0, PAIRS), (1, 0, 256), (1, 256, PAIRS)] if s == 0 else [(0, 0, PAIRS), (1, 0, PAIRS)]
+            for a, c0, c1 in parts:
                 cols = slice(N * a + P * s, N * a + P * (s + 1))
                 nc.tensor.matmul_mx(
-                    out=acc[:],
+                    out=acc[:, c0:c1],
                     lhsT=w2_codes[:, cols].bitcast(FP4X4),
                     lhsT_scale=w2_sc[:, cols],
-                    rhs=z_codes[a][:].bitcast(FP8X4),
-                    rhs_scale=z_sc[a][:],
+                    rhs=z_codes[a][:, c0:c1].bitcast(FP8X4),
+                    rhs_scale=z_sc[a][:, c0:c1],
                     start=(a == 0),
-                    stop=(a == 1),
+                    stop=(a == 1 and c1 == PAIRS),
                 )
             neg = ring.tile([P, PAIRS], F32, name="neg", bufs=4)
             nc.vector.scalar_tensor_tensor(
@@ -246,23 +278,28 @@ def tile_list_salt_screen_pairs_kernel(
             nc.scalar.activation(tanh[:], inland[:], ACT.Tanh, scale=-1.0)
             return tanh
 
-        def contrast(s, neg, tanh):
+        def contrast(s, neg, tanh, c0, c1):
             g, t = divmod(s, 4)
-            nc.vector.tensor_tensor(y32[g][:, t, :], neg[:].indirect(pos4_t[:]), tanh[:], ALU.add)
-
-        def hand_out(g, copy):
-            nc.sync.dma_start(out_0[512 * g : 512 * (g + 1), :].rearrange("(p t) j -> p t j", t=4), y32[g][:])
-            grouped = held([P, 4 * P2], BF16, f"y_grp{g}")
-            copy(
-                grouped[:].rearrange("p (c i t) -> p c t i", t=4, i=4),
-                y32[g][:].rearrange("p t (c i) -> p c t i", i=4),
+            nc.vector.tensor_tensor(
+                y32[g][:, t, c0:c1], neg[:].indirect(pos4_t[:, c0 // 16 : c1 // 16]), tanh[:, c0:c1], ALU.add
             )
-            return grouped
 
-        def planes(g, grouped):
+        def store_y(g, t0, t1):
+            rows = out_0[512 * g : 512 * (g + 1), :].rearrange("(p t) j -> p t j", t=4)
+            nc.sync.dma_start(rows[:, t0:t1, :], y32[g][:, t0:t1, :])
+
+        y_grp = [held([P, 4 * P2], BF16, f"y_grp{g}") for g in range(2)]
+
+        def round_y(g, c0, c1, copy):
+            copy(
+                y_grp[g][:, 4 * c0 : 4 * c1].rearrange("p (c i t) -> p c t i", t=4, i=4),
+                y32[g][:, :, c0:c1].rearrange("p t (c i) -> p c t i", i=4),
+            )
+
+        def planes(g):
             codes = held([P, P2], U32, f"y_codes{g}")
             scales = held([P, P2], U8, f"y_sc{g}")
-            nc.vector.quantize_mx(out=codes[:].bitcast(FP8X4), scales=scales[:], in_=grouped[:])
+            nc.vector.quantize_mx(out=codes[:].bitcast(FP8X4), scales=scales[:], in_=y_grp[g][:])
             nc.sync.dma_start(out_1[g].rearrange("p m t -> p (m t)").bitcast(I32), codes[:].bitcast(I32))
             for q in range(4):
                 queue = nc.scalar if (g == 1 and q >= 2) else nc.sync
@@ -272,15 +309,19 @@ def tile_list_salt_screen_pairs_kernel(
 
         negs = {0: minus_e(0), 1: minus_e(1)}
         tanhs = {0: bounded(negs[0])}
-        grouped0 = None
-        for s in range(8):
+        for s in range(7):
             if s + 2 < 8:
                 negs[s + 2] = minus_e(s + 2)
             if s + 1 < 8:
                 tanhs[s + 1] = bounded(negs[s + 1])
-            contrast(s, negs[s], tanhs[s])
+            contrast(s, negs[s], tanhs[s], 0, P2)
             if s == 3:
-                grouped0 = hand_out(0, nc.scalar.copy)
+                store_y(0, 0, 4)
+                round_y(0, 0, P2, nc.scalar.copy)
             if s == 5:
-                planes(0, grouped0)
-        planes(1, hand_out(1, nc.vector.tensor_copy))
+                planes(0)
+        store_y(1, 0, 3)
+        contrast(7, negs[7], tanhs[7], 0, P2)
+        store_y(1, 3, 4)
+        round_y(1, 0, P2, nc.vector.tensor_copy)
+        planes(1)

@@ -28,7 +28,7 @@ def tile_list_salt_screen_pairs_kernel(
     with ExitStack() as ctx:
         keep = ctx.enter_context(tc.tile_pool(name="keep", bufs=1))
         ring = ctx.enter_context(tc.tile_pool(name="ring", bufs=2))
-        psum = ctx.enter_context(tc.psum_pool(name="psum", bufs=8))
+        psum = ctx.enter_context(tc.psum_pool(name="psum", bufs=4))
 
         def held(shape, dtype, name):
             return keep.tile(shape, dtype, name=name, align_bytes=64)
@@ -54,30 +54,41 @@ def tile_list_salt_screen_pairs_kernel(
         nc.scalar.activation(warm[:, 1:2], warm[:, 0:1], ACT.Silu)
 
         tab_sc = held([P, T], U8, "tab_sc")
-        w2_sc_raw = held([P, 2 * N], U8, "w2_sc_raw")
-        nc.vector.memset(tab_sc[:].bitcast(I32), 0)
-        nc.vector.memset(w2_sc_raw[:].bitcast(I32), 0)
-        for q in range(4):
-            nc.gpsimd.dma_start(
-                tab_sc[32 * q : 32 * q + 8, :].bitcast(I32), tab_scales[:, 4 * q : 4 * q + 4, :].bitcast(I32)
-            )
+        w2_sc_raw = held([P, N], U8, "w2_sc_raw")
+        v_sc = [held([P, S], U8, f"v_sc{a}") for a in range(2)]
+        w2_sc = [held([P, N], U8, f"w2_sc{a}") for a in range(2)]
+        for tile in [tab_sc, w2_sc_raw] + v_sc + w2_sc:
+            nc.vector.memset(tile[:].bitcast(I32), 0)
+
+        def place_scale_rows(plane, spread, a, q):
+            first = 4 * (16 * a + 4 * q)
+            nc.sync.dma_start(plane[32 * q : 32 * q + 4, :].bitcast(I32), spread[first : first + 16 : 4, :].bitcast(I32))
 
         w1_raw = {(0, 0): [load_w1(0, 0, 0, 512)]}
         offs_t = load_list(offs, "offs_t")
+        nc.sync.dma_start(tab_sc[0:P:4, :].bitcast(I32), tab_scales.rearrange("a q c -> (a q) c").bitcast(I32))
+        nc.sync.dma_start(w2_sc_raw[0:P:4, :].bitcast(I32), w2_scales.rearrange("a q c -> (a q) c").bitcast(I32))
         gain_t = held([P, 2, 4], F32, "gain_t")
         nc.sync.dma_start(gain_t[:], gain.rearrange("(b p t) -> p b t", b=2, t=4))
-        for q in range(4):
-            nc.sync.dma_start(
-                w2_sc_raw[32 * q : 32 * q + 4, :].bitcast(I32).rearrange("r (a c) -> r a c", a=2),
-                w2_scales[:, 4 * q : 4 * q + 4, :].bitcast(I32).rearrange("a r c -> r a c"),
-            )
         w1_raw[0, 1] = [load_w1(0, 1, 0, 512)]
-        table = [load_table(0), load_table(1)]
+        v_sc_spread = held([P, S], U8, "v_sc_spread")
+        nc.vector.tensor_copy(v_sc_spread[:], tab_sc[:].indirect(offs_t[:]))
+        w2_sc_spread = held([P, N], U8, "w2_sc_spread")
+        nc.vector.tensor_copy(
+            w2_sc_spread[:].rearrange("p (g t m) -> p g t m", t=4, m=P),
+            w2_sc_raw[:].rearrange("p (g m t) -> p g t m", t=4, m=P),
+        )
+        table = [load_table(0)]
+        rows = [(a, q) for a in range(2) for q in range(4)]
+        for a, q in rows[:6]:
+            place_scale_rows(v_sc[a], v_sc_spread, a, q)
+        table.append(load_table(1))
+        for a, q in rows[6:]:
+            place_scale_rows(v_sc[a], v_sc_spread, a, q)
         pos1_t = load_list(pos1, "pos1_t")
         pos2_t = load_list(pos2, "pos2_t")
 
         v_words = [held([P, S], U32, f"v_words{a}") for a in range(2)]
-        v_sc = held([P, S], U8, "v_sc")
 
         w1_codes, w1_sc = {}, {}
 
@@ -115,6 +126,8 @@ def tile_list_salt_screen_pairs_kernel(
             tile = held([P, 4 * PAIRS], F32, f"pump{g}")
             nc.sync.dma_start(tile[:], pump[512 * g : 512 * (g + 1), :].rearrange("(p t) m -> p (t m)", t=4))
             pump_t.append(tile)
+        for a, q in rows:
+            place_scale_rows(w2_sc[a], w2_sc_spread, a, q)
         gain_sq = held([P, 8 * PAIRS], F32, "gain_sq")
         for s in range(8):
             nc.scalar.activation(
@@ -122,13 +135,7 @@ def tile_list_salt_screen_pairs_kernel(
                 gain_t[:, s // 4, s % 4 : s % 4 + 1].to_broadcast([P, PAIRS]),
                 ACT.Square,
             )
-        w2_sc = held([P, 2 * N], U8, "w2_sc")
-        nc.vector.tensor_copy(
-            w2_sc[:].rearrange("p (x t m) -> p x t m", t=4, m=P),
-            w2_sc_raw[:].rearrange("p (x m t) -> p x t m", t=4, m=P),
-        )
         quantize_w1(0, 0, grouped[0])
-        nc.vector.tensor_copy(v_sc[:], tab_sc[:].indirect(offs_t[:]))
         nc.vector.tensor_copy(v_words[0][:], table[0][:].indirect(offs_t[:]))
         quantize_w1(0, 1, grouped[1])
         for half in range(2):
@@ -155,7 +162,7 @@ def tile_list_salt_screen_pairs_kernel(
                         lhsT=w1_codes[b, a][:, P * t : P * (t + 1)].bitcast(FP8X4),
                         lhsT_scale=w1_sc[b, a][:, P * t : P * (t + 1)],
                         rhs=v_words[a][:, cols].bitcast(FP8X4),
-                        rhs_scale=v_sc[4 * a : P, cols],
+                        rhs_scale=v_sc[a][:, cols],
                         start=(a == 0),
                         stop=(a == 1),
                     )
@@ -234,9 +241,9 @@ def tile_list_salt_screen_pairs_kernel(
                 quantize_w1(1, 0, grouped)
             if s == -1:
                 quantize_w1(1, 1, round_w1(1, 1))
-            if s == 5:
+            if s == 4:
                 round_z(0, 0, PAIRS, nc.scalar.copy)
-            if s == 6:
+            if s == 5:
                 quantize_z(0, 0, PAIRS)
         pick(7, 0, 256)
         pair_product(6, 0, PAIRS)
@@ -252,14 +259,14 @@ def tile_list_salt_screen_pairs_kernel(
 
         def minus_e(s):
             g, t = divmod(s, 4)
-            acc = psum.tile([P, BANK], F32, name="acc")
+            acc = psum.tile([P, BANK], F32, name="acc" if g == 1 else "acc_early")
             parts = [(0, 0, PAIRS), (1, 0, 256), (1, 256, PAIRS)] if s == 0 else [(0, 0, PAIRS), (1, 0, PAIRS)]
             for a, c0, c1 in parts:
                 cols = slice(N * a + P * s, N * a + P * (s + 1))
                 nc.tensor.matmul_mx(
                     out=acc[:, c0:c1],
                     lhsT=w2_codes[:, cols].bitcast(FP4X4),
-                    lhsT_scale=w2_sc[:, cols],
+                    lhsT_scale=w2_sc[a][:, P * s : P * (s + 1)],
                     rhs=z_codes[a][:, c0:c1].bitcast(FP8X4),
                     rhs_scale=z_sc[a][:, c0:c1],
                     start=(a == 0),

@@ -3,7 +3,7 @@ from contextlib import ExitStack
 
 import concourse.mybir as mybir
 
-K, T, S, H, PAIRS, N, P2 = 1024, 4096, 1024, 1024, 512, 1024, 256
+K, T, S, H, PAIRS, N, WELLS = 1024, 4096, 1024, 1024, 512, 1024, 256
 FLOPS = 2 * K * H * S + 2 * H * N * PAIRS
 
 F32 = mybir.dt.float32
@@ -18,7 +18,16 @@ ALU = mybir.AluOpType
 ACT = mybir.ActivationFunctionType
 
 P = 128
+PACK = 4
+PASS = P * PACK
+PASSES = 2
+SLICES = PASSES * PACK
+QUADS = 4
 BANK = 512
+LIST_ROWS = 16
+HALF = PAIRS // 2
+DMAS_IN_FLIGHT = 8
+VECTOR_SHARE = 80
 
 
 def tile_list_salt_screen_pairs_kernel(
@@ -43,10 +52,10 @@ def tile_list_salt_screen_pairs_kernel(
             nc.sync.dma_start(tile[:].bitcast(I32), tab_words[a].rearrange("p t i -> p (t i)").bitcast(I32))
             return tile
 
-        def load_w1(b, a, c0, c1):
-            tile = ring.tile([P, 4, c1 - c0], F32, name="w1raw")
-            rows = w1[512 * a : 512 * (a + 1), 512 * b + c0 : 512 * b + c1]
-            nc.sync.dma_start(tile[:], rows.rearrange("(p j) c -> p j c", j=4))
+        def load_w1(b, a):
+            tile = ring.tile([P, PACK, PASS], F32, name="w1raw")
+            block = w1[PASS * a : PASS * (a + 1), PASS * b : PASS * (b + 1)]
+            nc.sync.dma_start(tile[:], block.rearrange("(p j) c -> p j c", j=PACK))
             return tile
 
         warm = held([P, 2], F32, "warm")
@@ -55,108 +64,115 @@ def tile_list_salt_screen_pairs_kernel(
 
         tab_sc = held([P, T], U8, "tab_sc")
         w2_sc_raw = held([P, N], U8, "w2_sc_raw")
-        v_sc = [held([P, S], U8, f"v_sc{a}") for a in range(2)]
-        w2_sc = [held([P, N], U8, f"w2_sc{a}") for a in range(2)]
+        v_sc = [held([P, S], U8, f"v_sc{a}") for a in range(PASSES)]
+        w2_sc = [held([P, N], U8, f"w2_sc{a}") for a in range(PASSES)]
         for tile in [tab_sc, w2_sc_raw] + v_sc + w2_sc:
             nc.vector.memset(tile[:].bitcast(I32), 0)
 
-        def place_scale_rows(plane, spread, a, q):
-            first = 4 * (16 * a + 4 * q)
-            nc.sync.dma_start(plane[32 * q : 32 * q + 4, :].bitcast(I32), spread[first : first + 16 : 4, :].bitcast(I32))
+        def place_scale_rows(plane, spread, a, quad):
+            first = 4 * (16 * a + 4 * quad)
+            nc.sync.dma_start(
+                plane[32 * quad : 32 * quad + 4, :].bitcast(I32), spread[first : first + 16 : 4, :].bitcast(I32)
+            )
 
-        w1_raw = {(0, 0): [load_w1(0, 0, 0, 512)]}
+        w1_raw = {(0, 0): load_w1(0, 0)}
         offs_t = load_list(offs, "offs_t")
         nc.sync.dma_start(tab_sc[0:P:4, :].bitcast(I32), tab_scales.rearrange("a q c -> (a q) c").bitcast(I32))
         nc.sync.dma_start(w2_sc_raw[0:P:4, :].bitcast(I32), w2_scales.rearrange("a q c -> (a q) c").bitcast(I32))
-        gain_t = held([P, 2, 4], F32, "gain_t")
-        nc.sync.dma_start(gain_t[:], gain.rearrange("(b p t) -> p b t", b=2, t=4))
-        w1_raw[0, 1] = [load_w1(0, 1, 0, 512)]
+        gain_t = held([P, PASSES, PACK], F32, "gain_t")
+        nc.sync.dma_start(gain_t[:], gain.rearrange("(b p t) -> p b t", b=PASSES, t=PACK))
         v_sc_spread = held([P, S], U8, "v_sc_spread")
         nc.vector.tensor_copy(v_sc_spread[:], tab_sc[:].indirect(offs_t[:]))
         w2_sc_spread = held([P, N], U8, "w2_sc_spread")
         nc.vector.tensor_copy(
-            w2_sc_spread[:].rearrange("p (g t m) -> p g t m", t=4, m=P),
-            w2_sc_raw[:].rearrange("p (g m t) -> p g t m", t=4, m=P),
+            w2_sc_spread[:].rearrange("p (g t m) -> p g t m", t=PACK, m=P),
+            w2_sc_raw[:].rearrange("p (g m t) -> p g t m", t=PACK, m=P),
         )
-        table = [load_table(0)]
-        rows = [(a, q) for a in range(2) for q in range(4)]
-        for a, q in rows[:6]:
-            place_scale_rows(v_sc[a], v_sc_spread, a, q)
-        table.append(load_table(1))
-        for a, q in rows[6:]:
-            place_scale_rows(v_sc[a], v_sc_spread, a, q)
-        pos1_t = load_list(pos1, "pos1_t")
-        pos2_t = load_list(pos2, "pos2_t")
+        table = [load_table(a) for a in range(PASSES)]
+        row_groups = [(a, quad) for a in range(PASSES) for quad in range(QUADS)]
+        ahead = DMAS_IN_FLIGHT - PASSES
+        for a, quad in row_groups[:ahead]:
+            place_scale_rows(v_sc[a], v_sc_spread, a, quad)
+        w1_raw[0, 1] = load_w1(0, 1)
+        for a, quad in row_groups[ahead:]:
+            place_scale_rows(v_sc[a], v_sc_spread, a, quad)
 
-        v_words = [held([P, S], U32, f"v_words{a}") for a in range(2)]
+        v_words = [held([P, S], U32, f"v_words{a}") for a in range(PASSES)]
 
         w1_codes, w1_sc = {}, {}
 
-        def round_w1(b, a):
-            if (b, a) == (1, 1):
-                grouped = keep.tile([P, 4 * 512], BF16, name="w1grp_last", tag="early", align_bytes=64)
-            else:
-                grouped = ring.tile([P, 4 * 512], BF16, name="w1grp", align_bytes=64)
-            dst = grouped[:].rearrange("p (t m j) -> p m t j", t=4, j=4)
-            pieces = w1_raw[b, a]
-            width = P // len(pieces)
-            for i, raw in enumerate(pieces):
-                src = raw[:].rearrange("p j (m t) -> p m t j", t=4)
-                copy = nc.vector.tensor_copy if b == 1 else nc.scalar.copy
-                copy(dst[:, width * i : width * (i + 1)], src)
+        def round_w1(b, a, on_vector):
+            grouped = ring.tile([P, PACK * PASS], BF16, name="w1grp", align_bytes=64)
+            dst = grouped[:].rearrange("p (t m j) -> p m t j", t=PACK, j=PACK)
+            src = w1_raw[b, a][:].rearrange("p j (m t) -> p m t j", t=PACK)
+            if on_vector > 0:
+                nc.vector.tensor_copy(dst[:, :on_vector], src[:, :on_vector])
+            if on_vector < P:
+                nc.scalar.copy(dst[:, on_vector:], src[:, on_vector:])
             return grouped
 
-        def quantize_w1(b, a, grouped):
-            w1_codes[b, a] = held([P, 512], U32, f"w1c{b}{a}")
-            w1_sc[b, a] = held([P, 512], U8, f"w1s{b}{a}")
-            nc.vector.quantize_mx(out=w1_codes[b, a][:].bitcast(FP8X4), scales=w1_sc[b, a][:], in_=grouped[:])
+        def quantize_w1(b, a, grouped, cuts):
+            w1_codes[b, a] = held([P, PASS], U32, f"w1c{b}{a}")
+            w1_sc[b, a] = held([P, PASS], U8, f"w1s{b}{a}")
+            for c0, c1 in zip(cuts, cuts[1:]):
+                nc.vector.quantize_mx(
+                    out=w1_codes[b, a][:, c0:c1].bitcast(FP8X4),
+                    scales=w1_sc[b, a][:, c0:c1],
+                    in_=grouped[:, PACK * c0 : PACK * c1],
+                )
 
-        grouped = [round_w1(0, a) for a in range(2)]
-        w1_raw[1, 0] = [load_w1(1, 0, 0, 512)]
-        w2_raw = held([P, 2 * N], U16, "w2_raw")
+        first_grouped = round_w1(0, 0, 0)
+
+        w2_raw = held([P, PASSES * N], U16, "w2_raw")
         nc.sync.dma_start(
-            w2_raw[:].bitcast(I32).rearrange("p (a c) -> p a c", a=2),
+            w2_raw[:].bitcast(I32).rearrange("p (a c) -> p a c", a=PASSES),
             w2_words.bitcast(I32).rearrange("a p c -> p a c"),
         )
-        w1_raw[1, 1] = [load_w1(1, 1, 0, 512)]
+        w1_raw[1, 0] = load_w1(1, 0)
+        w1_raw[1, 1] = load_w1(1, 1)
+        pos1_t = load_list(pos1, "pos1_t")
+        pos2_t = load_list(pos2, "pos2_t")
         pos3_t = load_list(pos3, "pos3_t")
         pos4_t = load_list(pos4, "pos4_t")
         pump_t = []
-        for g in range(2):
-            tile = held([P, 4 * PAIRS], F32, f"pump{g}")
-            nc.sync.dma_start(tile[:], pump[512 * g : 512 * (g + 1), :].rearrange("(p t) m -> p (t m)", t=4))
+        for g in range(PASSES):
+            tile = held([P, PACK * PAIRS], F32, f"pump{g}")
+            nc.sync.dma_start(tile[:], pump[PASS * g : PASS * (g + 1), :].rearrange("(p t) m -> p (t m)", t=PACK))
             pump_t.append(tile)
-        for a, q in rows:
-            place_scale_rows(w2_sc[a], w2_sc_spread, a, q)
-        gain_sq = held([P, 8 * PAIRS], F32, "gain_sq")
-        for s in range(8):
+        for a, quad in row_groups:
+            place_scale_rows(w2_sc[a], w2_sc_spread, a, quad)
+
+        gain_sq = held([P, SLICES * PAIRS], F32, "gain_sq")
+        for s in range(SLICES):
             nc.scalar.activation(
                 gain_sq[:, PAIRS * s : PAIRS * (s + 1)],
-                gain_t[:, s // 4, s % 4 : s % 4 + 1].to_broadcast([P, PAIRS]),
+                gain_t[:, s // PACK, s % PACK : s % PACK + 1].to_broadcast([P, PAIRS]),
                 ACT.Square,
             )
-        quantize_w1(0, 0, grouped[0])
-        nc.vector.tensor_copy(v_words[0][:], table[0][:].indirect(offs_t[:]))
-        quantize_w1(0, 1, grouped[1])
-        for half in range(2):
-            nc.vector.tensor_copy(
-                v_words[1][:, BANK * half : BANK * (half + 1)],
-                table[1][:].indirect(offs_t[:, 32 * half : 32 * (half + 1)]),
-            )
 
-        z_work = [held([P, 4 * S], F32, f"z_work{b}") for b in range(2)]
-        z_codes = [held([P, PAIRS], U32, f"z_codes{b}") for b in range(2)]
-        z_sc = [held([P, PAIRS], U8, f"z_sc{b}") for b in range(2)]
-        z_grp = [held([P, 4 * PAIRS], BF16, f"z_grp{b}") for b in range(2)]
-        turns, whole, rest, cosine, picked = {}, {}, {}, {}, {}
+        quantize_w1(0, 0, first_grouped, (0, PASS))
+        for a in range(PASSES):
+            nc.vector.tensor_copy(v_words[a][:], table[a][:].indirect(offs_t[:]))
+        quantize_w1(0, 1, round_w1(0, 1, VECTOR_SHARE), (0, P, PASS))
+        w2_codes = held([P, PASSES * N], U16, "w2_codes")
+        nc.vector.tensor_copy(
+            w2_codes[:].rearrange("p (x t m) -> p x t m", t=PACK, m=P),
+            w2_raw[:].rearrange("p (x m t) -> p x t m", t=PACK, m=P),
+        )
+
+        z_work = [held([P, PACK * S], F32, f"z_work{b}") for b in range(PASSES)]
+        z_codes = [held([P, PAIRS], U32, f"z_codes{b}") for b in range(PASSES)]
+        z_sc = [held([P, PAIRS], U8, f"z_sc{b}") for b in range(PASSES)]
+        z_grp = [held([P, PACK * PAIRS], BF16, f"z_grp{b}") for b in range(PASSES)]
+        turns, whole, reduced, cosine, shallow = {}, {}, {}, {}, {}
 
         def first_product(s):
-            b, t = divmod(s, 4)
+            b, t = divmod(s, PACK)
             turns[s] = ring.tile([P, S], F32, name="turns")
-            for half in range(2):
-                cols = slice(BANK * half, BANK * (half + 1))
+            for bank in range(S // BANK):
+                cols = slice(BANK * bank, BANK * (bank + 1))
                 acc = psum.tile([P, BANK], F32, name="acc")
-                for a in range(2):
+                for a in range(PASSES):
                     nc.tensor.matmul_mx(
                         out=acc[:],
                         lhsT=w1_codes[b, a][:, P * t : P * (t + 1)].bitcast(FP8X4),
@@ -164,171 +180,166 @@ def tile_list_salt_screen_pairs_kernel(
                         rhs=v_words[a][:, cols].bitcast(FP8X4),
                         rhs_scale=v_sc[a][:, cols],
                         start=(a == 0),
-                        stop=(a == 1),
+                        stop=(a == PASSES - 1),
                     )
                 nc.scalar.activation(turns[s][:, cols], acc[:], ACT.Abs, scale=0.5 / math.pi)
 
         def whole_turns(s):
-            if s == 0:
-                whole[s] = keep.tile([P, S], U32, name="whole_first", tag="early", align_bytes=64)
-            else:
-                whole[s] = ring.tile([P, S], U32, name="whole")
+            whole[s] = ring.tile([P, S], U32, name="whole")
             nc.scalar.activation(whole[s][:], turns[s][:], ACT.Copy, bias=0.25)
 
-        def remainder(s):
-            slot = (s - 1) % 8
-            rest[s] = z_work[slot // 4][:, S * (slot % 4) : S * (slot % 4 + 1)]
+        def reduce_angle(s):
+            b, t = divmod((s - 1) % SLICES, PACK)
+            reduced[s] = z_work[b][:, S * t : S * (t + 1)]
             nc.vector.scalar_tensor_tensor(
-                rest[s], turns[s][:], 0.25, whole[s][:].bitcast(I32), ALU.add, ALU.subtract
+                reduced[s], turns[s][:], 0.25, whole[s][:].bitcast(I32), ALU.add, ALU.subtract
             )
 
         def sine(s):
             cosine[s] = ring.tile([P, S], F32, name="cosine", bufs=3)
-            nc.scalar.activation(cosine[s][:], rest[s], ACT.Sin, scale=2.0 * math.pi)
+            nc.scalar.activation(cosine[s][:], reduced[s], ACT.Sin, scale=2.0 * math.pi)
 
-        def pick(s, c0, c1):
-            tile = ring.tile([P, c1 - c0], F32, name="shallow", bufs=3)
+        def pick_shallow(s, c0, c1):
+            shallow[s, c0] = ring.tile([P, c1 - c0], F32, name="shallow", bufs=3)
             nc.vector.tensor_tensor(
-                tile[:],
-                cosine[s][:].indirect(pos1_t[:, c0 // 16 : c1 // 16]),
+                shallow[s, c0][:],
+                cosine[s][:].indirect(pos1_t[:, c0 // LIST_ROWS : c1 // LIST_ROWS]),
                 gain_sq[:, PAIRS * s + c0 : PAIRS * s + c1],
                 ALU.mult,
             )
-            picked[s, c0] = tile
 
         def pair_product(s, c0, c1):
-            b, t = divmod(s, 4)
+            b, t = divmod(s, PACK)
             nc.vector.tensor_tensor(
                 z_work[b][:, S * t + c0 : S * t + c1],
-                cosine[s][:].indirect(pos2_t[:, c0 // 16 : c1 // 16]),
-                picked[s, c0][:],
+                cosine[s][:].indirect(pos2_t[:, c0 // LIST_ROWS : c1 // LIST_ROWS]),
+                shallow[s, c0][:],
                 ALU.mult,
             )
 
+        def interleave(copy, grouped, slices):
+            copy(
+                grouped.rearrange("p (c i t) -> p c t i", t=PACK, i=4),
+                slices.rearrange("p t (c i) -> p c t i", i=4),
+            )
+
         def round_z(b, c0, c1, copy):
-            dst = z_grp[b][:, 4 * c0 : 4 * c1].rearrange("p (c i t) -> p c t i", t=4, i=4)
-            src = z_work[b][:].rearrange("p (t m) -> p t m", t=4)[:, :, c0:c1]
-            copy(dst, src.rearrange("p t (c i) -> p c t i", i=4))
+            slices = z_work[b][:].rearrange("p (t m) -> p t m", t=PACK)[:, :, c0:c1]
+            interleave(copy, z_grp[b][:, PACK * c0 : PACK * c1], slices)
 
         def quantize_z(b, c0, c1):
             nc.vector.quantize_mx(
-                out=z_codes[b][:, c0:c1].bitcast(FP8X4), scales=z_sc[b][:, c0:c1], in_=z_grp[b][:, 4 * c0 : 4 * c1]
+                out=z_codes[b][:, c0:c1].bitcast(FP8X4),
+                scales=z_sc[b][:, c0:c1],
+                in_=z_grp[b][:, PACK * c0 : PACK * c1],
             )
 
-        w2_codes = held([P, 2 * N], U16, "w2_codes")
         first_product(0)
-        for s in range(-2, 7):
-            if s == -1:
-                sine(0)
-            if s + 2 < 8:
+        whole_turns(0)
+        first_product(1)
+        reduce_angle(0)
+        quantize_w1(1, 0, round_w1(1, 0, P), (0, PASS))
+        sine(0)
+        whole_turns(1)
+        first_product(2)
+        reduce_angle(1)
+        quantize_w1(1, 1, round_w1(1, 1, P), (0, PASS))
+        last = SLICES - 1
+        for s in range(last):
+            if s + 2 <= last:
                 whole_turns(s + 2)
-            if 0 < s + 1 < 8:
-                sine(s + 1)
-            if s + 3 < 8:
+            sine(s + 1)
+            if s + 3 <= last:
                 first_product(s + 3)
-            if s >= 0:
-                pick(s, 0, PAIRS)
-                if s >= 1:
-                    pair_product(s - 1, 0, PAIRS)
-            if s + 2 < 8:
-                remainder(s + 2)
-            if s == -2:
-                grouped = round_w1(1, 0)
-                nc.vector.tensor_copy(
-                    w2_codes[:].rearrange("p (x t m) -> p x t m", t=4, m=P),
-                    w2_raw[:].rearrange("p (x m t) -> p x t m", t=4, m=P),
-                )
-                quantize_w1(1, 0, grouped)
-            if s == -1:
-                quantize_w1(1, 1, round_w1(1, 1))
-            if s == 4:
+            pick_shallow(s, 0, PAIRS)
+            if s >= 1:
+                pair_product(s - 1, 0, PAIRS)
+            if s + 2 <= last:
+                reduce_angle(s + 2)
+            if s == PACK:
                 round_z(0, 0, PAIRS, nc.scalar.copy)
-            if s == 5:
+            if s == PACK + 1:
                 quantize_z(0, 0, PAIRS)
-        pick(7, 0, 256)
-        pair_product(6, 0, PAIRS)
-        pick(7, 256, PAIRS)
-        pair_product(7, 0, 256)
-        round_z(1, 0, 256, nc.scalar.copy)
-        pair_product(7, 256, PAIRS)
-        round_z(1, 256, PAIRS, nc.vector.tensor_copy)
-        quantize_z(1, 0, 256)
-        quantize_z(1, 256, PAIRS)
+        pick_shallow(last, 0, HALF)
+        pair_product(last - 1, 0, PAIRS)
+        pick_shallow(last, HALF, PAIRS)
+        pair_product(last, 0, HALF)
+        round_z(1, 0, HALF, nc.scalar.copy)
+        pair_product(last, HALF, PAIRS)
+        round_z(1, HALF, PAIRS, nc.vector.tensor_copy)
+        quantize_z(1, 0, HALF)
+        quantize_z(1, HALF, PAIRS)
 
-        y32 = [held([P, 4, P2], F32, f"y32_{g}") for g in range(2)]
+        y32 = [held([P, PACK, WELLS], F32, f"y32_{g}") for g in range(PASSES)]
 
-        def minus_e(s):
-            g, t = divmod(s, 4)
-            acc = psum.tile([P, BANK], F32, name="acc" if g == 1 else "acc_early")
-            parts = [(0, 0, PAIRS), (1, 0, 256), (1, 256, PAIRS)] if s == 0 else [(0, 0, PAIRS), (1, 0, PAIRS)]
-            for a, c0, c1 in parts:
-                cols = slice(N * a + P * s, N * a + P * (s + 1))
-                nc.tensor.matmul_mx(
-                    out=acc[:, c0:c1],
-                    lhsT=w2_codes[:, cols].bitcast(FP4X4),
-                    lhsT_scale=w2_sc[a][:, P * s : P * (s + 1)],
-                    rhs=z_codes[a][:, c0:c1].bitcast(FP8X4),
-                    rhs_scale=z_sc[a][:, c0:c1],
-                    start=(a == 0),
-                    stop=(a == 1 and c1 == PAIRS),
+        def second_product(s):
+            g, t = divmod(s, PACK)
+            minus_e = ring.tile([P, PAIRS], F32, name="neg", bufs=4)
+            cuts = (0, HALF, PAIRS) if s == 0 else (0, PAIRS)
+            for c0, c1 in zip(cuts, cuts[1:]):
+                acc = psum.tile([P, c1 - c0], F32, name="acc_early" if s <= 2 else "acc")
+                for a in range(PASSES):
+                    nc.tensor.matmul_mx(
+                        out=acc[:],
+                        lhsT=w2_codes[:, N * a + P * s : N * a + P * (s + 1)].bitcast(FP4X4),
+                        lhsT_scale=w2_sc[a][:, P * s : P * (s + 1)],
+                        rhs=z_codes[a][:, c0:c1].bitcast(FP8X4),
+                        rhs_scale=z_sc[a][:, c0:c1],
+                        start=(a == 0),
+                        stop=(a == PASSES - 1),
+                    )
+                nc.vector.scalar_tensor_tensor(
+                    minus_e[:, c0:c1],
+                    acc[:],
+                    -1.0,
+                    pump_t[g][:, PAIRS * t + c0 : PAIRS * t + c1],
+                    ALU.mult,
+                    ALU.subtract,
                 )
-            neg = ring.tile([P, PAIRS], F32, name="neg", bufs=4)
-            nc.vector.scalar_tensor_tensor(
-                neg[:], acc[:], -1.0, pump_t[g][:, PAIRS * t : PAIRS * (t + 1)], ALU.mult, ALU.subtract
-            )
-            return neg
+            return minus_e
 
-        def bounded(neg):
-            inland = ring.tile([P, P2], F32, name="inland")
-            nc.vector.tensor_copy(inland[:], neg[:].indirect(pos3_t[:]))
-            tanh = ring.tile([P, P2], F32, name="tanh", bufs=3)
-            nc.scalar.activation(tanh[:], inland[:], ACT.Tanh, scale=-1.0)
-            return tanh
+        def bound_inland(minus_e):
+            inland = ring.tile([P, WELLS], F32, name="inland")
+            nc.vector.tensor_copy(inland[:], minus_e[:].indirect(pos3_t[:]))
+            bounded = ring.tile([P, WELLS], F32, name="tanh", bufs=3)
+            nc.scalar.activation(bounded[:], inland[:], ACT.Tanh, scale=-1.0)
+            return bounded
 
-        def contrast(s, neg, tanh, c0, c1):
-            g, t = divmod(s, 4)
-            nc.vector.tensor_tensor(
-                y32[g][:, t, c0:c1], neg[:].indirect(pos4_t[:, c0 // 16 : c1 // 16]), tanh[:, c0:c1], ALU.add
-            )
+        def contrast(s, minus_e, bounded):
+            g, t = divmod(s, PACK)
+            nc.vector.tensor_tensor(y32[g][:, t, :], minus_e[:].indirect(pos4_t[:]), bounded[:], ALU.add)
 
         def store_y(g, t0, t1):
-            rows = out_0[512 * g : 512 * (g + 1), :].rearrange("(p t) j -> p t j", t=4)
+            rows = out_0[PASS * g : PASS * (g + 1), :].rearrange("(p t) j -> p t j", t=PACK)
             nc.sync.dma_start(rows[:, t0:t1, :], y32[g][:, t0:t1, :])
 
-        y_grp = [held([P, 4 * P2], BF16, f"y_grp{g}") for g in range(2)]
+        y_grp = [held([P, PACK * WELLS], BF16, f"y_grp{g}") for g in range(PASSES)]
 
-        def round_y(g, c0, c1, copy):
-            copy(
-                y_grp[g][:, 4 * c0 : 4 * c1].rearrange("p (c i t) -> p c t i", t=4, i=4),
-                y32[g][:, :, c0:c1].rearrange("p t (c i) -> p c t i", i=4),
-            )
-
-        def planes(g):
-            codes = held([P, P2], U32, f"y_codes{g}")
-            scales = held([P, P2], U8, f"y_sc{g}")
+        def store_planes(g, queues):
+            codes = held([P, WELLS], U32, f"y_codes{g}")
+            scales = held([P, WELLS], U8, f"y_sc{g}")
             nc.vector.quantize_mx(out=codes[:].bitcast(FP8X4), scales=scales[:], in_=y_grp[g][:])
             nc.sync.dma_start(out_1[g].rearrange("p m t -> p (m t)").bitcast(I32), codes[:].bitcast(I32))
-            for q in range(4):
-                queue = nc.scalar if (g == 1 and q >= 2) else nc.sync
+            for quad, queue in enumerate(queues):
                 queue.dma_start(
-                    out_2[g, 4 * q : 4 * q + 4, :].bitcast(I32), scales[32 * q : 32 * q + 4, :].bitcast(I32)
+                    out_2[g, 4 * quad : 4 * quad + 4, :].bitcast(I32),
+                    scales[32 * quad : 32 * quad + 4, :].bitcast(I32),
                 )
 
-        negs = {0: minus_e(0), 1: minus_e(1)}
-        tanhs = {0: bounded(negs[0])}
-        for s in range(7):
-            if s + 2 < 8:
-                negs[s + 2] = minus_e(s + 2)
-            if s + 1 < 8:
-                tanhs[s + 1] = bounded(negs[s + 1])
-            contrast(s, negs[s], tanhs[s], 0, P2)
-            if s == 3:
-                store_y(0, 0, 4)
-                round_y(0, 0, P2, nc.scalar.copy)
-            if s == 5:
-                planes(0)
-        store_y(1, 0, 3)
-        contrast(7, negs[7], tanhs[7], 0, P2)
-        store_y(1, 3, 4)
-        round_y(1, 0, P2, nc.vector.tensor_copy)
-        planes(1)
+        minus_es = {0: second_product(0), 1: second_product(1)}
+        boundeds = {0: bound_inland(minus_es[0])}
+        for s in range(last):
+            if s + 2 <= last:
+                minus_es[s + 2] = second_product(s + 2)
+            boundeds[s + 1] = bound_inland(minus_es[s + 1])
+            contrast(s, minus_es[s], boundeds[s])
+            if s == PACK - 1:
+                store_y(0, 0, PACK)
+                interleave(nc.scalar.copy, y_grp[0][:], y32[0][:])
+            if s == PACK + 1:
+                store_planes(0, [nc.sync] * QUADS)
+        store_y(1, 0, PACK - 1)
+        contrast(last, minus_es[last], boundeds[last])
+        store_y(1, PACK - 1, PACK)
+        interleave(nc.vector.tensor_copy, y_grp[1][:], y32[1][:])
+        store_planes(1, [nc.sync, nc.sync, nc.scalar, nc.scalar])

import math
from contextlib import ExitStack

import concourse.mybir as mybir

K, T, S, H, PAIRS, N, WELLS = 1024, 4096, 1024, 1024, 512, 1024, 256
FLOPS = 2 * K * H * S + 2 * H * N * PAIRS

F32 = mybir.dt.float32
BF16 = mybir.dt.bfloat16
I32 = mybir.dt.int32
U32 = mybir.dt.uint32
U16 = mybir.dt.uint16
U8 = mybir.dt.uint8
FP8X4 = mybir.dt.float8_e4m3fn_x4
FP4X4 = mybir.dt.float4_e2m1fn_x4
ALU = mybir.AluOpType
ACT = mybir.ActivationFunctionType

P = 128
PACK = 4
PASS = P * PACK
PASSES = 2
SLICES = PASSES * PACK
QUADS = 4
BANK = 512
LIST_ROWS = 16
HALF = PAIRS // 2
DMAS_IN_FLIGHT = 8
VECTOR_SHARE = 80


def tile_list_salt_screen_pairs_kernel(
    tc, tab_words, tab_scales, offs, pos1, pos2, pos3, pos4, w1, gain, w2_words, w2_scales, pump, out_0, out_1, out_2
):
    nc = tc.nc
    with ExitStack() as ctx:
        keep = ctx.enter_context(tc.tile_pool(name="keep", bufs=1))
        ring = ctx.enter_context(tc.tile_pool(name="ring", bufs=2))
        psum = ctx.enter_context(tc.psum_pool(name="psum", bufs=4))

        def held(shape, dtype, name):
            return keep.tile(shape, dtype, name=name, align_bytes=64)

        def load_list(src, name):
            tile = held([P, src.shape[1]], U16, name)
            nc.sync.dma_start(tile[:], src)
            return tile

        def load_table(a):
            tile = held([P, T], U32, f"table{a}")
            nc.sync.dma_start(tile[:].bitcast(I32), tab_words[a].rearrange("p t i -> p (t i)").bitcast(I32))
            return tile

        def load_w1(b, a):
            tile = ring.tile([P, PACK, PASS], F32, name="w1raw")
            block = w1[PASS * a : PASS * (a + 1), PASS * b : PASS * (b + 1)]
            nc.sync.dma_start(tile[:], block.rearrange("(p j) c -> p j c", j=PACK))
            return tile

        warm = held([P, 2], F32, "warm")
        nc.gpsimd.memset(warm[:, 0:1], 0.0)
        nc.scalar.activation(warm[:, 1:2], warm[:, 0:1], ACT.Silu)

        tab_sc = held([P, T], U8, "tab_sc")
        w2_sc_raw = held([P, N], U8, "w2_sc_raw")
        v_sc = [held([P, S], U8, f"v_sc{a}") for a in range(PASSES)]
        w2_sc = [held([P, N], U8, f"w2_sc{a}") for a in range(PASSES)]
        for tile in [tab_sc, w2_sc_raw] + v_sc + w2_sc:
            nc.vector.memset(tile[:].bitcast(I32), 0)

        def place_scale_rows(plane, spread, a, quad):
            first = 4 * (16 * a + 4 * quad)
            nc.sync.dma_start(
                plane[32 * quad : 32 * quad + 4, :].bitcast(I32), spread[first : first + 16 : 4, :].bitcast(I32)
            )

        w1_raw = {(0, 0): load_w1(0, 0)}
        offs_t = load_list(offs, "offs_t")
        nc.sync.dma_start(tab_sc[0:P:4, :].bitcast(I32), tab_scales.rearrange("a q c -> (a q) c").bitcast(I32))
        nc.sync.dma_start(w2_sc_raw[0:P:4, :].bitcast(I32), w2_scales.rearrange("a q c -> (a q) c").bitcast(I32))
        gain_t = held([P, PASSES, PACK], F32, "gain_t")
        nc.sync.dma_start(gain_t[:], gain.rearrange("(b p t) -> p b t", b=PASSES, t=PACK))
        v_sc_spread = held([P, S], U8, "v_sc_spread")
        nc.vector.tensor_copy(v_sc_spread[:], tab_sc[:].indirect(offs_t[:]))
        w2_sc_spread = held([P, N], U8, "w2_sc_spread")
        nc.vector.tensor_copy(
            w2_sc_spread[:].rearrange("p (g t m) -> p g t m", t=PACK, m=P),
            w2_sc_raw[:].rearrange("p (g m t) -> p g t m", t=PACK, m=P),
        )
        table = [load_table(a) for a in range(PASSES)]
        row_groups = [(a, quad) for a in range(PASSES) for quad in range(QUADS)]
        ahead = DMAS_IN_FLIGHT - PASSES
        for a, quad in row_groups[:ahead]:
            place_scale_rows(v_sc[a], v_sc_spread, a, quad)
        w1_raw[0, 1] = load_w1(0, 1)
        for a, quad in row_groups[ahead:]:
            place_scale_rows(v_sc[a], v_sc_spread, a, quad)

        v_words = [held([P, S], U32, f"v_words{a}") for a in range(PASSES)]

        w1_codes, w1_sc = {}, {}

        def round_w1(b, a, on_vector):
            grouped = ring.tile([P, PACK * PASS], BF16, name="w1grp", align_bytes=64)
            dst = grouped[:].rearrange("p (t m j) -> p m t j", t=PACK, j=PACK)
            src = w1_raw[b, a][:].rearrange("p j (m t) -> p m t j", t=PACK)
            if on_vector > 0:
                nc.vector.tensor_copy(dst[:, :on_vector], src[:, :on_vector])
            if on_vector < P:
                nc.scalar.copy(dst[:, on_vector:], src[:, on_vector:])
            return grouped

        def quantize_w1(b, a, grouped, cuts):
            w1_codes[b, a] = held([P, PASS], U32, f"w1c{b}{a}")
            w1_sc[b, a] = held([P, PASS], U8, f"w1s{b}{a}")
            for c0, c1 in zip(cuts, cuts[1:]):
                nc.vector.quantize_mx(
                    out=w1_codes[b, a][:, c0:c1].bitcast(FP8X4),
                    scales=w1_sc[b, a][:, c0:c1],
                    in_=grouped[:, PACK * c0 : PACK * c1],
                )

        first_grouped = round_w1(0, 0, 0)

        w2_raw = held([P, PASSES * N], U16, "w2_raw")
        nc.sync.dma_start(
            w2_raw[:].bitcast(I32).rearrange("p (a c) -> p a c", a=PASSES),
            w2_words.bitcast(I32).rearrange("a p c -> p a c"),
        )
        w1_raw[1, 0] = load_w1(1, 0)
        w1_raw[1, 1] = load_w1(1, 1)
        pos1_t = load_list(pos1, "pos1_t")
        pos2_t = load_list(pos2, "pos2_t")
        pos3_t = load_list(pos3, "pos3_t")
        pos4_t = load_list(pos4, "pos4_t")
        pump_t = []
        for g in range(PASSES):
            tile = held([P, PACK * PAIRS], F32, f"pump{g}")
            nc.sync.dma_start(tile[:], pump[PASS * g : PASS * (g + 1), :].rearrange("(p t) m -> p (t m)", t=PACK))
            pump_t.append(tile)
        for a, quad in row_groups:
            place_scale_rows(w2_sc[a], w2_sc_spread, a, quad)

        gain_sq = held([P, SLICES * PAIRS], F32, "gain_sq")
        for s in range(SLICES):
            nc.scalar.activation(
                gain_sq[:, PAIRS * s : PAIRS * (s + 1)],
                gain_t[:, s // PACK, s % PACK : s % PACK + 1].to_broadcast([P, PAIRS]),
                ACT.Square,
            )

        quantize_w1(0, 0, first_grouped, (0, PASS))
        for a in range(PASSES):
            nc.vector.tensor_copy(v_words[a][:], table[a][:].indirect(offs_t[:]))
        quantize_w1(0, 1, round_w1(0, 1, VECTOR_SHARE), (0, P, PASS))
        w2_codes = held([P, PASSES * N], U16, "w2_codes")
        nc.vector.tensor_copy(
            w2_codes[:].rearrange("p (x t m) -> p x t m", t=PACK, m=P),
            w2_raw[:].rearrange("p (x m t) -> p x t m", t=PACK, m=P),
        )

        z_work = [held([P, PACK * S], F32, f"z_work{b}") for b in range(PASSES)]
        z_codes = [held([P, PAIRS], U32, f"z_codes{b}") for b in range(PASSES)]
        z_sc = [held([P, PAIRS], U8, f"z_sc{b}") for b in range(PASSES)]
        z_grp = [held([P, PACK * PAIRS], BF16, f"z_grp{b}") for b in range(PASSES)]
        turns, whole, reduced, cosine, shallow = {}, {}, {}, {}, {}

        def first_product(s):
            b, t = divmod(s, PACK)
            turns[s] = ring.tile([P, S], F32, name="turns")
            for bank in range(S // BANK):
                cols = slice(BANK * bank, BANK * (bank + 1))
                acc = psum.tile([P, BANK], F32, name="acc")
                for a in range(PASSES):
                    nc.tensor.matmul_mx(
                        out=acc[:],
                        lhsT=w1_codes[b, a][:, P * t : P * (t + 1)].bitcast(FP8X4),
                        lhsT_scale=w1_sc[b, a][:, P * t : P * (t + 1)],
                        rhs=v_words[a][:, cols].bitcast(FP8X4),
                        rhs_scale=v_sc[a][:, cols],
                        start=(a == 0),
                        stop=(a == PASSES - 1),
                    )
                nc.scalar.activation(turns[s][:, cols], acc[:], ACT.Abs, scale=0.5 / math.pi)

        def whole_turns(s):
            whole[s] = ring.tile([P, S], U32, name="whole")
            nc.scalar.activation(whole[s][:], turns[s][:], ACT.Copy, bias=0.25)

        def reduce_angle(s):
            b, t = divmod((s - 1) % SLICES, PACK)
            reduced[s] = z_work[b][:, S * t : S * (t + 1)]
            nc.vector.scalar_tensor_tensor(
                reduced[s], turns[s][:], 0.25, whole[s][:].bitcast(I32), ALU.add, ALU.subtract
            )

        def sine(s):
            cosine[s] = ring.tile([P, S], F32, name="cosine", bufs=3)
            nc.scalar.activation(cosine[s][:], reduced[s], ACT.Sin, scale=2.0 * math.pi)

        def pick_shallow(s, c0, c1):
            shallow[s, c0] = ring.tile([P, c1 - c0], F32, name="shallow", bufs=3)
            nc.vector.tensor_tensor(
                shallow[s, c0][:],
                cosine[s][:].indirect(pos1_t[:, c0 // LIST_ROWS : c1 // LIST_ROWS]),
                gain_sq[:, PAIRS * s + c0 : PAIRS * s + c1],
                ALU.mult,
            )

        def pair_product(s, c0, c1):
            b, t = divmod(s, PACK)
            nc.vector.tensor_tensor(
                z_work[b][:, S * t + c0 : S * t + c1],
                cosine[s][:].indirect(pos2_t[:, c0 // LIST_ROWS : c1 // LIST_ROWS]),
                shallow[s, c0][:],
                ALU.mult,
            )

        def interleave(copy, grouped, slices):
            copy(
                grouped.rearrange("p (c i t) -> p c t i", t=PACK, i=4),
                slices.rearrange("p t (c i) -> p c t i", i=4),
            )

        def round_z(b, c0, c1, copy):
            slices = z_work[b][:].rearrange("p (t m) -> p t m", t=PACK)[:, :, c0:c1]
            interleave(copy, z_grp[b][:, PACK * c0 : PACK * c1], slices)

        def quantize_z(b, c0, c1):
            nc.vector.quantize_mx(
                out=z_codes[b][:, c0:c1].bitcast(FP8X4),
                scales=z_sc[b][:, c0:c1],
                in_=z_grp[b][:, PACK * c0 : PACK * c1],
            )

        first_product(0)
        whole_turns(0)
        first_product(1)
        reduce_angle(0)
        quantize_w1(1, 0, round_w1(1, 0, P), (0, PASS))
        sine(0)
        whole_turns(1)
        first_product(2)
        reduce_angle(1)
        quantize_w1(1, 1, round_w1(1, 1, P), (0, PASS))
        last = SLICES - 1
        for s in range(last):
            if s + 2 <= last:
                whole_turns(s + 2)
            sine(s + 1)
            if s + 3 <= last:
                first_product(s + 3)
            pick_shallow(s, 0, PAIRS)
            if s >= 1:
                pair_product(s - 1, 0, PAIRS)
            if s + 2 <= last:
                reduce_angle(s + 2)
            if s == PACK:
                round_z(0, 0, PAIRS, nc.scalar.copy)
            if s == PACK + 1:
                quantize_z(0, 0, PAIRS)
        pick_shallow(last, 0, HALF)
        pair_product(last - 1, 0, PAIRS)
        pick_shallow(last, HALF, PAIRS)
        pair_product(last, 0, HALF)
        round_z(1, 0, HALF, nc.scalar.copy)
        pair_product(last, HALF, PAIRS)
        round_z(1, HALF, PAIRS, nc.vector.tensor_copy)
        quantize_z(1, 0, HALF)
        quantize_z(1, HALF, PAIRS)

        y32 = [held([P, PACK, WELLS], F32, f"y32_{g}") for g in range(PASSES)]

        def second_product(s):
            g, t = divmod(s, PACK)
            minus_e = ring.tile([P, PAIRS], F32, name="neg", bufs=4)
            cuts = (0, HALF, PAIRS) if s == 0 else (0, PAIRS)
            for c0, c1 in zip(cuts, cuts[1:]):
                acc = psum.tile([P, c1 - c0], F32, name="acc_early" if s <= 2 else "acc")
                for a in range(PASSES):
                    nc.tensor.matmul_mx(
                        out=acc[:],
                        lhsT=w2_codes[:, N * a + P * s : N * a + P * (s + 1)].bitcast(FP4X4),
                        lhsT_scale=w2_sc[a][:, P * s : P * (s + 1)],
                        rhs=z_codes[a][:, c0:c1].bitcast(FP8X4),
                        rhs_scale=z_sc[a][:, c0:c1],
                        start=(a == 0),
                        stop=(a == PASSES - 1),
                    )
                nc.vector.scalar_tensor_tensor(
                    minus_e[:, c0:c1],
                    acc[:],
                    -1.0,
                    pump_t[g][:, PAIRS * t + c0 : PAIRS * t + c1],
                    ALU.mult,
                    ALU.subtract,
                )
            return minus_e

        def bound_inland(minus_e):
            inland = ring.tile([P, WELLS], F32, name="inland")
            nc.vector.tensor_copy(inland[:], minus_e[:].indirect(pos3_t[:]))
            bounded = ring.tile([P, WELLS], F32, name="tanh", bufs=3)
            nc.scalar.activation(bounded[:], inland[:], ACT.Tanh, scale=-1.0)
            return bounded

        def contrast(s, minus_e, bounded):
            g, t = divmod(s, PACK)
            nc.vector.tensor_tensor(y32[g][:, t, :], minus_e[:].indirect(pos4_t[:]), bounded[:], ALU.add)

        def store_y(g, t0, t1):
            rows = out_0[PASS * g : PASS * (g + 1), :].rearrange("(p t) j -> p t j", t=PACK)
            nc.sync.dma_start(rows[:, t0:t1, :], y32[g][:, t0:t1, :])

        y_grp = [held([P, PACK * WELLS], BF16, f"y_grp{g}") for g in range(PASSES)]

        def store_planes(g, queues):
            codes = held([P, WELLS], U32, f"y_codes{g}")
            scales = held([P, WELLS], U8, f"y_sc{g}")
            nc.vector.quantize_mx(out=codes[:].bitcast(FP8X4), scales=scales[:], in_=y_grp[g][:])
            nc.sync.dma_start(out_1[g].rearrange("p m t -> p (m t)").bitcast(I32), codes[:].bitcast(I32))
            for quad, queue in enumerate(queues):
                queue.dma_start(
                    out_2[g, 4 * quad : 4 * quad + 4, :].bitcast(I32),
                    scales[32 * quad : 32 * quad + 4, :].bitcast(I32),
                )

        minus_es = {0: second_product(0), 1: second_product(1)}
        boundeds = {0: bound_inland(minus_es[0])}
        for s in range(last):
            if s + 2 <= last:
                minus_es[s + 2] = second_product(s + 2)
            boundeds[s + 1] = bound_inland(minus_es[s + 1])
            contrast(s, minus_es[s], boundeds[s])
            if s == PACK - 1:
                store_y(0, 0, PACK)
                interleave(nc.scalar.copy, y_grp[0][:], y32[0][:])
            if s == PACK + 1:
                store_planes(0, [nc.sync] * QUADS)
        store_y(1, 0, PACK - 1)
        contrast(last, minus_es[last], boundeds[last])
        store_y(1, PACK - 1, PACK)
        interleave(nc.vector.tensor_copy, y_grp[1][:], y32[1][:])
        store_planes(1, [nc.sync, nc.sync, nc.scalar, nc.scalar])
